import numpy as np
import ml_dtypes


def mxq(x, axis, fmt="e4m3"):
    dtype, down = {"e4m3": (ml_dtypes.float8_e4m3fn, 7), "e5m2": (ml_dtypes.float8_e5m2, 14)}[fmt]
    v = np.moveaxis(np.asarray(x, np.float32).astype(ml_dtypes.bfloat16).astype(np.float64), axis, -1)
    blocks = v.reshape(v.shape[:-1] + (-1, 32))
    amax = np.abs(blocks).max(-1, keepdims=True)
    byte = np.maximum(np.where(amax > 0, np.frexp(amax)[1] - 1 + 127, 0) - down, 1)
    scale = np.exp2(byte - 127.0)
    codes = (blocks / scale).astype(np.float32).astype(dtype).astype(np.float64)
    return np.moveaxis((codes * scale).reshape(v.shape), -1, axis)


WIDE = False


def mx_kscale(k):
    if not WIDE:
        return np.ones(k)
    levels = np.array([10, -10, 5, -5, 0])
    if k % 512:
        return np.exp2(np.random.permutation(np.resize(levels, k // 32))).repeat(32)
    a = np.empty((k // 512, 16))
    for p in range(k // 512):
        a[p, :8] = np.random.permutation(np.resize(levels, 8))
        for g in range(8):
            far = levels[np.abs(levels - a[p, g]) >= 10]
            a[p, g + 8] = far[np.random.randint(len(far))]
    return np.exp2(a.ravel()).repeat(32)


def f64(x):
    return np.asarray(x).astype(np.float64)


def striped(idx):
    return np.tile(idx.reshape(-1, 16).T, (8, 1)).astype(np.uint16)


def unstriped(offs):
    return offs[:16].T.reshape(-1).astype(np.int64)


def pack_weight(w):
    k, n = w.shape
    w = f64(np.asarray(w, np.float32).astype(ml_dtypes.bfloat16)).reshape(k // 32, 32, n)
    amax = np.abs(w).max(1)
    byte = np.clip(np.where(amax > 0, np.frexp(amax)[1] - 1 + 127 - 7, 1), 1, 254)
    scaled = (w * np.exp2(127.0 - byte)[:, None, :]).reshape(k, n).astype(np.float32)
    words = np.ascontiguousarray(scaled.reshape(k // 512, 128, 4, n).transpose(0, 1, 3, 2)).astype(ml_dtypes.float8_e4m3fn).view(np.uint8)
    return words, np.ascontiguousarray(byte.astype(np.uint8).reshape(k // 512, 16, n))


def unpack_weight(words, scales):
    g, p, n, _ = words.shape
    vals = np.ascontiguousarray(words).view(ml_dtypes.float8_e4m3fn).astype(np.float64) * np.repeat(np.exp2(scales.astype(np.float64) - 127.0), 8, axis=1)[..., None]
    return vals.transpose(0, 1, 3, 2).reshape(g * 512, n)


E2M1 = np.array([0.0, 0.5, 1.0, 1.5, 2.0, 3.0, 4.0, 6.0, -0.0, -0.5, -1.0, -1.5, -2.0, -3.0, -4.0, -6.0])


def pack_fp4(w):
    k, n = w.shape
    w = f64(np.asarray(w, np.float32).astype(ml_dtypes.bfloat16)).reshape(k // 32, 32, n)
    amax = np.abs(w).max(1)
    mant, ex = np.frexp(amax / 6.0)
    byte = np.clip(np.where(amax > 0, np.where(mant > 0.5, ex, ex - 1) + 127, 1), 1, 254)
    scaled = (w * np.exp2(127.0 - byte)[:, None, :]).reshape(k, n).astype(np.float32)
    c = np.ascontiguousarray(scaled.reshape(k // 512, 128, 4, n).transpose(0, 1, 3, 2)).astype(ml_dtypes.float4_e2m1fn).view(np.uint8) & 0xF
    words = (c[..., 0::2] | (c[..., 1::2] << 4)).reshape(k // 512, 128, 2 * n)
    return np.ascontiguousarray(words), np.ascontiguousarray(byte.astype(np.uint8).reshape(k // 512, 16, n))


def unpack_fp4(words, scales):
    g, _, n = scales.shape
    words = np.ascontiguousarray(words).reshape(g, 128, n, 2)
    nib = np.empty((g, 128, n, 4), np.uint8)
    nib[..., 0::2] = words & 0xF
    nib[..., 1::2] = words >> 4
    vals = E2M1[nib] * np.repeat(np.exp2(scales.astype(np.float64) - 127.0), 8, axis=1)[..., None]
    return vals.transpose(0, 1, 3, 2).reshape(g * 512, n)


K, T, S, N, H = 1024, 1024, 512, 128, 512


def setup_inputs():
    n = np.random.standard_normal
    s = mx_kscale(K)[:, None]
    u = mx_kscale(H)
    packed_xT = pack_weight(n((K, T)) * s)
    packed_w1 = pack_fp4(n((K, H)) / np.sqrt(K) / s)
    packed_w2 = pack_fp4(n((K, H)) / np.sqrt(K) / s)
    packed_w3 = pack_fp4(n((H, N)) / np.sqrt(H) / u[:, None])
    return {
        "x_words": packed_xT[0],
        "x_scales": packed_xT[1],
        "w1_words": packed_w1[0],
        "w1_scales": packed_w1[1],
        "w2_words": packed_w2[0],
        "w2_scales": packed_w2[1],
        "eps": (np.random.uniform(0.3, 2.0, (H, S))).astype(np.float32),
        "unit": (np.random.uniform(0.6, 1.4, (H, 1)) * u[:, None]).astype(np.float32),
        "w3_words": packed_w3[0],
        "w3_scales": packed_w3[1],
        "offs": striped(np.random.permutation(T)[:S]),
        "prv": striped(np.random.permutation(S)),
    }


def reference(x_words, x_scales, w1_words, w1_scales, w2_words, w2_scales, eps, unit, w3_words, w3_scales, offs, prv):
    xq = unpack_weight(x_words, x_scales)[:, unstriped(offs)]
    y = unpack_fp4(w1_words, w1_scales).T @ xq
    psi = 0.8 * (np.log(np.exp(y) + 1.0)) + 0.2
    pp = psi[:, unstriped(prv)]
    dur = pp * f64(eps)
    psin = 0.3 * dur + 0.5 * psi + 0.1
    haz = np.sqrt(dur) / psin
    vo = unpack_fp4(w2_words, w2_scales).T @ xq
    volu = (np.log(np.exp(vo) + 1.0)) * (haz / (haz + 0.7))
    vp = volu[:, unstriped(prv)]
    hid = f64(unit) * (haz * vp)
    return unpack_fp4(w3_words, w3_scales).T @ mxq(hid, 0, "e4m3")

@@ -1,0 +1,247 @@
+import math
+from contextlib import ExitStack
+
+import concourse.mybir as mybir
+from concourse.masks import make_identity
+
+F32 = mybir.dt.float32
+BF16 = mybir.dt.bfloat16
+I32 = mybir.dt.int32
+U32 = mybir.dt.uint32
+U16 = mybir.dt.uint16
+U8 = mybir.dt.uint8
+FP8X4 = mybir.dt.float8_e4m3fn_x4
+FP4X4 = mybir.dt.float4_e2m1fn_x4
+ACT = mybir.ActivationFunctionType
+ALU = mybir.AluOpType
+
+K, T, S, N, H = 1024, 1024, 512, 128, 512
+P = 128
+PACK = 4
+PASSES = K // (P * PACK)
+QUADS = 4
+BLOCKS = S // P
+HALF = S // 2
+FLOPS = 2 * (2 * K * H * S) + 2 * H * N * S
+
+KNEE = 30.0
+PSI_SHIFT = 0.25
+
+
+def tile_picked_yacddu_haz_p_kernel(
+    tc, x_words, x_scales, w1_words, w1_scales, w2_words, w2_scales, eps, unit, w3_words, w3_scales, offs, prv, out
+):
+    nc = tc.nc
+    with ExitStack() as ctx:
+        lists = ctx.enter_context(tc.tile_pool(name="lists", bufs=1))
+        sb = ctx.enter_context(tc.tile_pool(name="sb", bufs=1))
+        psum = ctx.enter_context(tc.psum_pool(name="psum", bufs=1))
+
+        def bank(b, name):
+            return psum.tile([P, S], F32, name=name, tag="bank%d" % b)
+
+        def load_scale_rows(queue, plane, scales):
+            for q in range(QUADS):
+                queue.dma_start(
+                    out=plane[32 * q : 32 * q + 4].bitcast(I32),
+                    in_=scales[:, 4 * q : 4 * q + 4, :].rearrange("o r c -> r o c").bitcast(I32),
+                )
+
+        offs_sb = lists.tile([P, S // 16], U16, name="offs_sb")
+        prv_sb = lists.tile([P, S // 16], U16, name="prv_sb")
+        xw = [sb.tile([P, T], U32, name="xw%d" % o) for o in range(PASSES)]
+        xs = sb.tile([P, PASSES, T], U8, name="xs", tag="xs")
+        ww = [sb.tile([P, PASSES, 2 * H], U8, name="ww%d" % i, align_bytes=64) for i in range(2)]
+        ws = [sb.tile([P, PASSES, H], U8, name="ws%d" % i, align_bytes=64) for i in range(2)]
+        ident = sb.tile([P, P], F32, name="ident")
+
+        nc.gpsimd.memset(xs[:].bitcast(I32), 0)
+        for plane in ws:
+            nc.vector.memset(plane[:].bitcast(I32), 0)
+
+        def load_x_words(o):
+            nc.sync.dma_start(
+                out=xw[o][:].bitcast(I32), in_=x_words[o].rearrange("p c r -> p (c r)").bitcast(I32)
+            )
+
+        nc.sync.dma_start(offs_sb[:], offs)
+        load_scale_rows(nc.sync, xs, x_scales)
+        for o in range(PASSES):
+            load_x_words(o)
+        for i, (words, scales) in enumerate(((w1_words, w1_scales), (w2_words, w2_scales))):
+            nc.sync.dma_start(out=ww[i][:].bitcast(I32), in_=words.rearrange("o p c -> p o c").bitcast(I32))
+            load_scale_rows(nc.sync, ws[i], scales)
+        nc.sync.dma_start(prv_sb[:], prv)
+        make_identity(nc, ident[:])
+
+        def dealt(ap):
+            return ap.rearrange("p (m t) -> p t m", t=PACK)
+
+        e1 = [sb.tile([P, PACK, P], F32, name="e1_%d" % b) for b in range(BLOCKS)]
+        r1 = [sb.tile([P, PACK, P], F32, name="r1_%d" % b) for b in range(BLOCKS)]
+        r2 = [sb.tile([P, PACK, P], F32, name="r2_%d" % b) for b in range(BLOCKS)]
+        l2 = [sb.tile([P, PACK, P], F32, name="l2_%d" % b) for b in range(BLOCKS)]
+        e2 = sb.tile([P, BLOCKS, PACK, P], F32, name="e2")
+
+        gs = [sb.tile([P, S], U8, name="gs%d" % o, align_bytes=64) for o in range(PASSES)]
+        for o in range(PASSES):
+            nc.vector.tensor_copy(gs[o][:], xs[:, o, :].indirect(offs_sb[:]))
+        gw = []
+        for b in range(BLOCKS):
+            picks = offs_sb[:, b * (P // 16) : (b + 1) * (P // 16)]
+            gw.append([])
+            for o in range(PASSES):
+                gw[b].append(sb.tile([P, P], U32, name="gw%d_%d" % (b, o), tag="gw%d_%d" % (b, o), align_bytes=64))
+                nc.vector.tensor_copy(gw[b][o][:], xw[o][:].indirect(picks))
+
+        def product(acc, i, b):
+            for o in range(PASSES):
+                nc.tensor.matmul_mx(
+                    acc[:],
+                    lhsT=gw[b][o][:].bitcast(FP8X4),
+                    lhsT_scale=gs[o][:, b * P : (b + 1) * P],
+                    rhs=ww[i][:, o, :].bitcast(FP4X4),
+                    rhs_scale=ws[i][:, o, :],
+                    start=(o == 0),
+                    stop=(o == PASSES - 1),
+                )
+
+        y_bank = [bank(b, "y_%d" % b) for b in range(BLOCKS)]
+        v_bank = [bank(BLOCKS + b, "v_%d" % b) for b in range(BLOCKS)]
+        for b in range(BLOCKS):
+            product(y_bank[b], 0, b)
+            nc.scalar.activation(e1[b][:], dealt(y_bank[b][:]), ACT.Exp)
+            nc.gpsimd.tensor_scalar(e1[b][:], e1[b][:], math.exp(KNEE), 0.0, ALU.min, ALU.max)
+        for b in range(BLOCKS):
+            product(v_bank[b], 1, b)
+            nc.scalar.activation(e2[:, b], dealt(v_bank[b][:]), ACT.Exp)
+
+        eps_sb = sb.tile([P, PACK, S], F32, name="eps_sb", tag="xs")
+        nc.sync.dma_start(out=eps_sb[:], in_=eps.rearrange("(p t) j -> p t j", t=PACK))
+
+        w3w = sb.tile([P, 2 * N], U8, name="w3w", tag="gw0_0", align_bytes=64)
+        w3s = sb.tile([P, 1, N], U8, name="w3s", tag="gw0_1", align_bytes=64)
+        unit_sb = sb.tile([P, PACK], F32, name="unit_sb", tag="gw1_0", align_bytes=64)
+        nc.sync.dma_start(out=unit_sb[:], in_=unit.rearrange("(p t) o -> p (t o)", t=PACK))
+        nc.sync.dma_start(out=w3w[:].bitcast(I32), in_=w3_words[0].bitcast(I32))
+        nc.gpsimd.memset(w3s[:].bitcast(I32), 0)
+        load_scale_rows(nc.sync, w3s, w3_scales)
+
+        nc.gpsimd.tensor_scalar(e2[:], e2[:], math.exp(KNEE), 0.0, ALU.min, ALU.max)
+        for b in range(BLOCKS):
+            nc.vector.tensor_scalar(r1[b][:], dealt(y_bank[b][:]), -KNEE, 0.0, ALU.add, ALU.max)
+        for b in range(BLOCKS):
+            nc.vector.tensor_scalar(r2[b][:], dealt(v_bank[b][:]), -KNEE, 0.0, ALU.add, ALU.max)
+
+        def turn(dst, t, *sources):
+            for b in range(BLOCKS):
+                for i, src in enumerate(sources):
+                    nc.tensor.matmul(
+                        dst[:, b * P : (b + 1) * P],
+                        lhsT=src[b][:, t, :],
+                        rhs=ident[:],
+                        is_transpose=True,
+                        start=(i == 0),
+                        stop=(i == len(sources) - 1),
+                    )
+
+        shift = math.exp(PSI_SHIFT)
+        e_bank = [bank(t, "e_%d" % t) for t in range(PACK)]
+        r_bank = [bank(BLOCKS + t, "r_%d" % t) for t in range(PACK)]
+        psi = [sb.tile([P, 2 * S], F32, name="psi%d" % t, tag="psi%d" % t) for t in range(PACK)]
+        dur = [sb.tile([P, S], F32, name="dur%d" % t) for t in range(PACK)]
+        mix = [sb.tile([P, S], F32, name="mix%d" % t) for t in range(PACK)]
+        for t in range(PACK):
+            turn(e_bank[t], t, e1)
+            turn(r_bank[t], t, r1)
+            nc.scalar.activation(psi[t][:, S:], e_bank[t][:], ACT.Ln, bias=shift, scale=shift)
+        for step in range(PACK + 2):
+            if step < PACK:
+                t = step
+                nc.vector.tensor_tensor(psi[t][:, :S], r_bank[t][:], psi[t][:, S:], ALU.add)
+            if 1 <= step <= PACK:
+                t = step - 1
+                nc.vector.tensor_tensor(dur[t][:], psi[t][:].indirect(prv_sb[:]), eps_sb[:, t, :], ALU.mult)
+            if step >= 2:
+                t = step - 2
+                nc.vector.scalar_tensor_tensor(mix[t][:], dur[t][:], 0.6, psi[t][:, :S], ALU.mult, ALU.add)
+
+        for b in range(BLOCKS):
+            nc.scalar.activation(l2[b][:], e2[:, b], ACT.Ln, bias=1.0)
+        s_bank = []
+        for t in range(PACK):
+            s_bank.append(bank(t, "s_%d" % t))
+            turn(s_bank[t], t, r2, l2)
+
+        ln_dur, ln_psin = [], []
+        for t in range(PACK):
+            ln_dur.append(sb.tile([P, S], F32, name="ln_dur%d" % t, tag="ln_dur%d" % t))
+            ln_psin.append(sb.tile([P, S], F32, name="ln_psin%d" % t))
+            nc.scalar.activation(ln_dur[t][:], dur[t][:], ACT.Ln, bias=2.0**-63, scale=0.8)
+            nc.scalar.activation(ln_psin[t][:], mix[t][:], ACT.Ln, bias=0.1, scale=0.4)
+
+        ln_haz = []
+        for t in range(PACK):
+            tag = "psi%d" % (PACK - 1) if t == 0 else "ln_dur%d" % (t - 1)
+            ln_haz.append(sb.tile([P, S], F32, name="ln_haz%d" % t, tag=tag))
+            nc.vector.scalar_tensor_tensor(ln_haz[t][:], ln_dur[t][:], 0.5, ln_psin[t][:], ALU.mult, ALU.subtract)
+
+        hv = sb.tile([P, PACK, S], F32, name="hv")
+        volu = [sb.tile([P, 2 * S], F32, name="volu%d" % t) for t in range(PACK)]
+        haz = [sb.tile([P, S], F32, name="haz%d" % t) for t in range(PACK)]
+
+        def gate(t):
+            nc.scalar.activation(volu[t][:, S:], ln_haz[t][:], ACT.Tanh, bias=-0.5 * math.log(0.7), scale=0.5)
+            nc.vector.scalar_tensor_tensor(volu[t][:, :S], volu[t][:, S:], 1.0, s_bank[t][:], ALU.add, ALU.mult)
+
+        def hazard(t):
+            nc.scalar.activation(haz[t][:], ln_haz[t][:], ACT.Exp, bias=-math.log(2.0))
+
+        def fetch_on_vector(t):
+            nc.gpsimd.tensor_scalar(haz[t][:], haz[t][:], unit_sb[:, t : t + 1], 0.0, ALU.mult, ALU.add)
+            nc.vector.tensor_tensor(hv[:, t, :], volu[t][:].indirect(prv_sb[:]), haz[t][:], ALU.mult)
+
+        def fetch_on_scalar(t):
+            vp = sb.tile([P, S], F32, name="vp%d" % t)
+            nc.scalar.activation(vp[:], volu[t][:].indirect(prv_sb[:]), ACT.Copy)
+            nc.vector.scalar_tensor_tensor(hv[:, t, :], vp[:], unit_sb[:, t : t + 1], haz[t][:], ALU.mult, ALU.mult)
+
+        for t in (0, 1):
+            gate(t)
+            hazard(t)
+        fetch_on_vector(0)
+        for t in (2, 3):
+            gate(t)
+        fetch_on_vector(1)
+        for t in (2, 3):
+            hazard(t)
+        for t in (2, 3):
+            fetch_on_scalar(t)
+
+        hid = []
+        for h in range(2):
+            cols = slice(h * HALF, (h + 1) * HALF)
+            hid.append(sb.tile([P, HALF * PACK], BF16, name="hid%d" % h, align_bytes=64))
+            weave = nc.vector.tensor_copy if h == 0 else nc.scalar.copy
+            weave(
+                hid[h][:].rearrange("p (c i t) -> p c t i", i=4, t=PACK),
+                hv[:, :, cols].rearrange("p t (c i) -> p c t i", i=4),
+            )
+        for h in range(2):
+            cols = slice(h * HALF, (h + 1) * HALF)
+            codes = sb.tile([P, HALF], U32, name="codes%d" % h, align_bytes=64)
+            plane = sb.tile([P, HALF], U8, name="plane%d" % h, align_bytes=64)
+            nc.vector.quantize_mx(codes[:].bitcast(FP8X4), plane[:], hid[h][:])
+            o_bank = bank(BLOCKS + h, "o_%d" % h)
+            nc.tensor.matmul_mx(
+                o_bank[:, :HALF],
+                lhsT=w3w[:].bitcast(FP4X4),
+                lhsT_scale=w3s[:, 0, :],
+                rhs=codes[:].bitcast(FP8X4),
+                rhs_scale=plane[:],
+                start=True,
+                stop=True,
+            )
+            res = sb.tile([P, HALF], F32, name="res%d" % h)
+            nc.scalar.copy(res[:], o_bank[:, :HALF])
+            nc.sync.dma_start(out=out[:, cols], in_=res[:])

@@ -64,14 +64,22 @@ def tile_picked_yacddu_haz_p_kernel(
                 out=xw[o][:].bitcast(I32), in_=x_words[o].rearrange("p c r -> p (c r)").bitcast(I32)
             )
 
+        def load_w_words(i, words):
+            nc.sync.dma_start(out=ww[i][:].bitcast(I32), in_=words.rearrange("o p c -> p o c").bitcast(I32))
+
         nc.sync.dma_start(offs_sb[:], offs)
         load_scale_rows(nc.sync, xs, x_scales)
-        for o in range(PASSES):
-            load_x_words(o)
-        for i, (words, scales) in enumerate(((w1_words, w1_scales), (w2_words, w2_scales))):
-            nc.sync.dma_start(out=ww[i][:].bitcast(I32), in_=words.rearrange("o p c -> p o c").bitcast(I32))
-            load_scale_rows(nc.sync, ws[i], scales)
+        load_x_words(0)
+        load_w_words(0, w1_words)
+        load_x_words(1)
+        load_scale_rows(nc.sync, ws[0], w1_scales)
+        load_w_words(1, w2_words)
+        load_scale_rows(nc.sync, ws[1], w2_scales)
         nc.sync.dma_start(prv_sb[:], prv)
+        unit_sb = sb.tile([P, PACK], F32, name="unit_sb")
+        half_unit = sb.tile([P, PACK], F32, name="half_unit")
+        nc.gpsimd.dma_start(out=unit_sb[:], in_=unit.rearrange("(p t) o -> p (t o)", t=PACK))
+        nc.scalar.activation(half_unit[:], unit_sb[:], ACT.Identity, scale=0.5)
         make_identity(nc, ident[:])
 
         def dealt(ap):
@@ -84,36 +92,47 @@ def tile_picked_yacddu_haz_p_kernel(
         e2 = sb.tile([P, BLOCKS, PACK, P], F32, name="e2")
 
         gs = [sb.tile([P, S], U8, name="gs%d" % o, align_bytes=64) for o in range(PASSES)]
+        gw = [
+            [sb.tile([P, P], U32, name="gw%d_%d" % (b, o), tag="gw%d_%d" % (b, o), align_bytes=64) for o in range(PASSES)]
+            for b in range(BLOCKS)
+        ]
+
+        def pick_words(b, o):
+            nc.vector.tensor_copy(gw[b][o][:], xw[o][:].indirect(offs_sb[:, b * (P // 16) : (b + 1) * (P // 16)]))
+
         for o in range(PASSES):
             nc.vector.tensor_copy(gs[o][:], xs[:, o, :].indirect(offs_sb[:]))
-        gw = []
-        for b in range(BLOCKS):
-            picks = offs_sb[:, b * (P // 16) : (b + 1) * (P // 16)]
-            gw.append([])
+            for b in (0, 1):
+                pick_words(b, o)
+        for b in (2, 3):
             for o in range(PASSES):
-                gw[b].append(sb.tile([P, P], U32, name="gw%d_%d" % (b, o), tag="gw%d_%d" % (b, o), align_bytes=64))
-                nc.vector.tensor_copy(gw[b][o][:], xw[o][:].indirect(picks))
+                pick_words(b, o)
 
-        def product(acc, i, b):
-            for o in range(PASSES):
-                nc.tensor.matmul_mx(
-                    acc[:],
-                    lhsT=gw[b][o][:].bitcast(FP8X4),
-                    lhsT_scale=gs[o][:, b * P : (b + 1) * P],
-                    rhs=ww[i][:, o, :].bitcast(FP4X4),
-                    rhs_scale=ws[i][:, o, :],
-                    start=(o == 0),
-                    stop=(o == PASSES - 1),
-                )
+        def mx_pass(acc, i, b, o):
+            nc.tensor.matmul_mx(
+                acc[:],
+                lhsT=gw[b][o][:].bitcast(FP8X4),
+                lhsT_scale=gs[o][:, b * P : (b + 1) * P],
+                rhs=ww[i][:, o, :].bitcast(FP4X4),
+                rhs_scale=ws[i][:, o, :],
+                start=(o == 0),
+                stop=(o == PASSES - 1),
+            )
 
         y_bank = [bank(b, "y_%d" % b) for b in range(BLOCKS)]
         v_bank = [bank(BLOCKS + b, "v_%d" % b) for b in range(BLOCKS)]
+        for o in range(PASSES):
+            for b in (0, 1):
+                mx_pass(y_bank[b], 0, b, o)
+        for b in (2, 3):
+            for o in range(PASSES):
+                mx_pass(y_bank[b], 0, b, o)
         for b in range(BLOCKS):
-            product(y_bank[b], 0, b)
             nc.scalar.activation(e1[b][:], dealt(y_bank[b][:]), ACT.Exp)
             nc.gpsimd.tensor_scalar(e1[b][:], e1[b][:], math.exp(KNEE), 0.0, ALU.min, ALU.max)
         for b in range(BLOCKS):
-            product(v_bank[b], 1, b)
+            for o in range(PASSES):
+                mx_pass(v_bank[b], 1, b, o)
             nc.scalar.activation(e2[:, b], dealt(v_bank[b][:]), ACT.Exp)
 
         eps_sb = sb.tile([P, PACK, S], F32, name="eps_sb", tag="xs")
@@ -121,8 +140,6 @@ def tile_picked_yacddu_haz_p_kernel(
 
         w3w = sb.tile([P, 2 * N], U8, name="w3w", tag="gw0_0", align_bytes=64)
         w3s = sb.tile([P, 1, N], U8, name="w3s", tag="gw0_1", align_bytes=64)
-        unit_sb = sb.tile([P, PACK], F32, name="unit_sb", tag="gw1_0", align_bytes=64)
-        nc.sync.dma_start(out=unit_sb[:], in_=unit.rearrange("(p t) o -> p (t o)", t=PACK))
         nc.sync.dma_start(out=w3w[:].bitcast(I32), in_=w3_words[0].bitcast(I32))
         nc.gpsimd.memset(w3s[:].bitcast(I32), 0)
         load_scale_rows(nc.sync, w3s, w3_scales)
@@ -132,6 +149,20 @@ def tile_picked_yacddu_haz_p_kernel(
             nc.vector.tensor_scalar(r1[b][:], dealt(y_bank[b][:]), -KNEE, 0.0, ALU.add, ALU.max)
         for b in range(BLOCKS):
             nc.vector.tensor_scalar(r2[b][:], dealt(v_bank[b][:]), -KNEE, 0.0, ALU.add, ALU.max)
+
+        nc.vector.tensor_scalar(eps_sb[:], eps_sb[:], 0.6, None, ALU.mult)
+
+        def flip(dst, src, start, stop):
+            for b in range(BLOCKS):
+                cols = slice(b * P, (b + 1) * P)
+                nc.tensor.matmul(
+                    dst[:, cols],
+                    lhsT=src[:, cols],
+                    rhs=ident[:],
+                    is_transpose=True,
+                    start=(start and b == 0),
+                    stop=(stop and b == BLOCKS - 1),
+                )
 
         def turn(dst, t, *sources):
             for b in range(BLOCKS):
@@ -150,35 +181,38 @@ def tile_picked_yacddu_haz_p_kernel(
         r_bank = [bank(BLOCKS + t, "r_%d" % t) for t in range(PACK)]
         psi = [sb.tile([P, 2 * S], F32, name="psi%d" % t, tag="psi%d" % t) for t in range(PACK)]
         dur = [sb.tile([P, S], F32, name="dur%d" % t) for t in range(PACK)]
-        mix = [sb.tile([P, S], F32, name="mix%d" % t) for t in range(PACK)]
+        mix = []
         for t in range(PACK):
             turn(e_bank[t], t, e1)
             turn(r_bank[t], t, r1)
             nc.scalar.activation(psi[t][:, S:], e_bank[t][:], ACT.Ln, bias=shift, scale=shift)
-        for step in range(PACK + 2):
+        for step in range(PACK + 1):
             if step < PACK:
                 t = step
                 nc.vector.tensor_tensor(psi[t][:, :S], r_bank[t][:], psi[t][:, S:], ALU.add)
-            if 1 <= step <= PACK:
+                mix.append(bank(BLOCKS + t, "mix_%d" % t))
+                flip(mix[t], psi[t], True, False)
+            if step >= 1:
                 t = step - 1
                 nc.vector.tensor_tensor(dur[t][:], psi[t][:].indirect(prv_sb[:]), eps_sb[:, t, :], ALU.mult)
-            if step >= 2:
-                t = step - 2
-                nc.vector.scalar_tensor_tensor(mix[t][:], dur[t][:], 0.6, psi[t][:, :S], ALU.mult, ALU.add)
+                flip(mix[t], dur[t], False, True)
 
         for b in range(BLOCKS):
             nc.scalar.activation(l2[b][:], e2[:, b], ACT.Ln, bias=1.0)
-        s_bank = []
-        for t in range(PACK):
-            s_bank.append(bank(t, "s_%d" % t))
-            turn(s_bank[t], t, r2, l2)
 
         ln_dur, ln_psin = [], []
         for t in range(PACK):
             ln_dur.append(sb.tile([P, S], F32, name="ln_dur%d" % t, tag="ln_dur%d" % t))
-            ln_psin.append(sb.tile([P, S], F32, name="ln_psin%d" % t))
-            nc.scalar.activation(ln_dur[t][:], dur[t][:], ACT.Ln, bias=2.0**-63, scale=0.8)
-            nc.scalar.activation(ln_psin[t][:], mix[t][:], ACT.Ln, bias=0.1, scale=0.4)
+            flipped = sb.tile([P, S], F32, name="flipped%d" % t)
+            nc.scalar.activation(ln_dur[t][:], dur[t][:], ACT.Ln, bias=2.0**-63, scale=0.8 / 0.6)
+            nc.scalar.activation(flipped[:], mix[t][:], ACT.Ln, bias=0.1, scale=0.4)
+            ln_psin.append(bank(BLOCKS + t, "ln_psin%d" % t))
+            flip(ln_psin[t], flipped, True, True)
+
+        s_bank = []
+        for t in range(PACK):
+            s_bank.append(bank(t, "s_%d" % t))
+            turn(s_bank[t], t, r2, l2)
 
         ln_haz = []
         for t in range(PACK):
@@ -195,40 +229,31 @@ def tile_picked_yacddu_haz_p_kernel(
             nc.vector.scalar_tensor_tensor(volu[t][:, :S], volu[t][:, S:], 1.0, s_bank[t][:], ALU.add, ALU.mult)
 
         def hazard(t):
-            nc.scalar.activation(haz[t][:], ln_haz[t][:], ACT.Exp, bias=-math.log(2.0))
+            nc.scalar.activation(haz[t][:], ln_haz[t][:], ACT.Exp)
 
         def fetch_on_vector(t):
-            nc.gpsimd.tensor_scalar(haz[t][:], haz[t][:], unit_sb[:, t : t + 1], 0.0, ALU.mult, ALU.add)
+            nc.gpsimd.tensor_scalar(haz[t][:], haz[t][:], half_unit[:, t : t + 1], 0.0, ALU.mult, ALU.add)
             nc.vector.tensor_tensor(hv[:, t, :], volu[t][:].indirect(prv_sb[:]), haz[t][:], ALU.mult)
 
-        def fetch_on_scalar(t):
-            vp = sb.tile([P, S], F32, name="vp%d" % t)
-            nc.scalar.activation(vp[:], volu[t][:].indirect(prv_sb[:]), ACT.Copy)
-            nc.vector.scalar_tensor_tensor(hv[:, t, :], vp[:], unit_sb[:, t : t + 1], haz[t][:], ALU.mult, ALU.mult)
+        vp = {t: sb.tile([P, S], F32, name="vp%d" % t) for t in (2, 3)}
 
-        for t in (0, 1):
-            gate(t)
-            hazard(t)
-        fetch_on_vector(0)
-        for t in (2, 3):
-            gate(t)
-        fetch_on_vector(1)
-        for t in (2, 3):
-            hazard(t)
-        for t in (2, 3):
-            fetch_on_scalar(t)
-
-        hid = []
-        for h in range(2):
+        def fetch_on_scalar(t, h):
             cols = slice(h * HALF, (h + 1) * HALF)
-            hid.append(sb.tile([P, HALF * PACK], BF16, name="hid%d" % h, align_bytes=64))
-            weave = nc.vector.tensor_copy if h == 0 else nc.scalar.copy
-            weave(
-                hid[h][:].rearrange("p (c i t) -> p c t i", i=4, t=PACK),
-                hv[:, :, cols].rearrange("p t (c i) -> p c t i", i=4),
+            picks = prv_sb[:, h * (HALF // 16) : (h + 1) * (HALF // 16)]
+            nc.scalar.activation(vp[t][:, cols], volu[t][:].indirect(picks), ACT.Copy)
+            nc.vector.scalar_tensor_tensor(
+                hv[:, t, cols], vp[t][:, cols], half_unit[:, t : t + 1], haz[t][:, cols], ALU.mult, ALU.mult
             )
-        for h in range(2):
-            cols = slice(h * HALF, (h + 1) * HALF)
+
+        hid = [sb.tile([P, HALF * PACK], BF16, name="hid%d" % h, align_bytes=64) for h in range(2)]
+
+        def weave(copy, h, first, count):
+            copy(
+                hid[h][:, first * PACK : (first + count) * PACK].rearrange("p (c i t) -> p c t i", i=4, t=PACK),
+                hv[:, :, h * HALF + first : h * HALF + first + count].rearrange("p t (c i) -> p c t i", i=4),
+            )
+
+        def finish(h):
             codes = sb.tile([P, HALF], U32, name="codes%d" % h, align_bytes=64)
             plane = sb.tile([P, HALF], U8, name="plane%d" % h, align_bytes=64)
             nc.vector.quantize_mx(codes[:].bitcast(FP8X4), plane[:], hid[h][:])
@@ -244,4 +269,23 @@ def tile_picked_yacddu_haz_p_kernel(
             )
             res = sb.tile([P, HALF], F32, name="res%d" % h)
             nc.scalar.copy(res[:], o_bank[:, :HALF])
-            nc.sync.dma_start(out=out[:, cols], in_=res[:])
+            nc.sync.dma_start(out=out[:, h * HALF : (h + 1) * HALF], in_=res[:])
+
+        for t in (0, 1):
+            hazard(t)
+            gate(t)
+        fetch_on_vector(0)
+        for t in (2, 3):
+            gate(t)
+        fetch_on_vector(1)
+        for t in (2, 3):
+            hazard(t)
+        for t in (2, 3):
+            fetch_on_scalar(t, 0)
+        fetch_on_scalar(2, 1)
+        weave(nc.vector.tensor_copy, 0, 0, HALF)
+        fetch_on_scalar(3, 1)
+        finish(0)
+        weave(nc.scalar.copy, 1, 0, HALF // 2)
+        weave(nc.vector.tensor_copy, 1, HALF // 2, HALF // 2)
+        finish(1)

@@ -49,37 +49,35 @@ def tile_picked_yacddu_haz_p_kernel(
 
         offs_sb = lists.tile([P, S // 16], U16, name="offs_sb")
         prv_sb = lists.tile([P, S // 16], U16, name="prv_sb")
-        xw = [sb.tile([P, T], U32, name="xw%d" % o) for o in range(PASSES)]
+        xw = sb.tile([P, PASSES, T], U32, name="xw")
         xs = sb.tile([P, PASSES, T], U8, name="xs", tag="xs")
         ww = [sb.tile([P, PASSES, 2 * H], U8, name="ww%d" % i, align_bytes=64) for i in range(2)]
         ws = [sb.tile([P, PASSES, H], U8, name="ws%d" % i, align_bytes=64) for i in range(2)]
+        w3w = sb.tile([P, 2 * N], U8, name="w3w", align_bytes=64)
+        w3s = sb.tile([P, 1, N], U8, name="w3s", align_bytes=64)
+        unit_sb = sb.tile([P, PACK], F32, name="unit_sb")
+        eps_sb = sb.tile([P, PACK, S], F32, name="eps_sb")
         ident = sb.tile([P, P], F32, name="ident")
 
         nc.gpsimd.memset(xs[:].bitcast(I32), 0)
-        for plane in ws:
+        for plane in (ws[0], ws[1], w3s):
             nc.vector.memset(plane[:].bitcast(I32), 0)
-
-        def load_x_words(o):
-            nc.sync.dma_start(
-                out=xw[o][:].bitcast(I32), in_=x_words[o].rearrange("p c r -> p (c r)").bitcast(I32)
-            )
 
         def load_w_words(i, words):
             nc.sync.dma_start(out=ww[i][:].bitcast(I32), in_=words.rearrange("o p c -> p o c").bitcast(I32))
 
         nc.sync.dma_start(offs_sb[:], offs)
+        nc.sync.dma_start(prv_sb[:], prv)
+        nc.sync.dma_start(out=w3w[:].bitcast(I32), in_=w3_words[0].bitcast(I32))
         load_scale_rows(nc.sync, xs, x_scales)
-        load_x_words(0)
+        nc.sync.dma_start(out=xw[:].bitcast(I32), in_=x_words.rearrange("o p c r -> p o (c r)").bitcast(I32))
         load_w_words(0, w1_words)
-        load_x_words(1)
         load_scale_rows(nc.sync, ws[0], w1_scales)
         load_w_words(1, w2_words)
         load_scale_rows(nc.sync, ws[1], w2_scales)
-        nc.sync.dma_start(prv_sb[:], prv)
-        unit_sb = sb.tile([P, PACK], F32, name="unit_sb")
-        half_unit = sb.tile([P, PACK], F32, name="half_unit")
-        nc.gpsimd.dma_start(out=unit_sb[:], in_=unit.rearrange("(p t) o -> p (t o)", t=PACK))
-        nc.scalar.activation(half_unit[:], unit_sb[:], ACT.Identity, scale=0.5)
+        nc.sync.dma_start(out=eps_sb[:], in_=eps.rearrange("(p t) j -> p t j", t=PACK))
+        nc.sync.dma_start(out=unit_sb[:], in_=unit.rearrange("(p t) o -> p (t o)", t=PACK))
+        load_scale_rows(nc.sync, w3s, w3_scales)
         make_identity(nc, ident[:])
 
         def dealt(ap):
@@ -98,13 +96,11 @@ def tile_picked_yacddu_haz_p_kernel(
         ]
 
         def pick_words(b, o):
-            nc.vector.tensor_copy(gw[b][o][:], xw[o][:].indirect(offs_sb[:, b * (P // 16) : (b + 1) * (P // 16)]))
+            nc.vector.tensor_copy(gw[b][o][:], xw[:, o, :].indirect(offs_sb[:, b * (P // 16) : (b + 1) * (P // 16)]))
 
         for o in range(PASSES):
             nc.vector.tensor_copy(gs[o][:], xs[:, o, :].indirect(offs_sb[:]))
-            for b in (0, 1):
-                pick_words(b, o)
-        for b in (2, 3):
+        for b in range(BLOCKS):
             for o in range(PASSES):
                 pick_words(b, o)
 
@@ -121,29 +117,15 @@ def tile_picked_yacddu_haz_p_kernel(
 
         y_bank = [bank(b, "y_%d" % b) for b in range(BLOCKS)]
         v_bank = [bank(BLOCKS + b, "v_%d" % b) for b in range(BLOCKS)]
-        for o in range(PASSES):
-            for b in (0, 1):
-                mx_pass(y_bank[b], 0, b, o)
-        for b in (2, 3):
+        for b in range(BLOCKS):
             for o in range(PASSES):
                 mx_pass(y_bank[b], 0, b, o)
-        for b in range(BLOCKS):
             nc.scalar.activation(e1[b][:], dealt(y_bank[b][:]), ACT.Exp)
             nc.gpsimd.tensor_scalar(e1[b][:], e1[b][:], math.exp(KNEE), 0.0, ALU.min, ALU.max)
         for b in range(BLOCKS):
             for o in range(PASSES):
                 mx_pass(v_bank[b], 1, b, o)
             nc.scalar.activation(e2[:, b], dealt(v_bank[b][:]), ACT.Exp)
-
-        eps_sb = sb.tile([P, PACK, S], F32, name="eps_sb", tag="xs")
-        nc.sync.dma_start(out=eps_sb[:], in_=eps.rearrange("(p t) j -> p t j", t=PACK))
-
-        w3w = sb.tile([P, 2 * N], U8, name="w3w", tag="gw0_0", align_bytes=64)
-        w3s = sb.tile([P, 1, N], U8, name="w3s", tag="gw0_1", align_bytes=64)
-        nc.sync.dma_start(out=w3w[:].bitcast(I32), in_=w3_words[0].bitcast(I32))
-        nc.gpsimd.memset(w3s[:].bitcast(I32), 0)
-        load_scale_rows(nc.sync, w3s, w3_scales)
-
         nc.gpsimd.tensor_scalar(e2[:], e2[:], math.exp(KNEE), 0.0, ALU.min, ALU.max)
         for b in range(BLOCKS):
             nc.vector.tensor_scalar(r1[b][:], dealt(y_bank[b][:]), -KNEE, 0.0, ALU.add, ALU.max)
@@ -209,16 +191,16 @@ def tile_picked_yacddu_haz_p_kernel(
             ln_psin.append(bank(BLOCKS + t, "ln_psin%d" % t))
             flip(ln_psin[t], flipped, True, True)
 
-        s_bank = []
-        for t in range(PACK):
-            s_bank.append(bank(t, "s_%d" % t))
-            turn(s_bank[t], t, r2, l2)
-
         ln_haz = []
         for t in range(PACK):
             tag = "psi%d" % (PACK - 1) if t == 0 else "ln_dur%d" % (t - 1)
             ln_haz.append(sb.tile([P, S], F32, name="ln_haz%d" % t, tag=tag))
             nc.vector.scalar_tensor_tensor(ln_haz[t][:], ln_dur[t][:], 0.5, ln_psin[t][:], ALU.mult, ALU.subtract)
+
+        s_bank = []
+        for t in range(PACK):
+            s_bank.append(bank(BLOCKS + t, "s_%d" % t))
+            turn(s_bank[t], t, r2, l2)
 
         hv = sb.tile([P, PACK, S], F32, name="hv")
         volu = [sb.tile([P, 2 * S], F32, name="volu%d" % t) for t in range(PACK)]
@@ -229,10 +211,10 @@ def tile_picked_yacddu_haz_p_kernel(
             nc.vector.scalar_tensor_tensor(volu[t][:, :S], volu[t][:, S:], 1.0, s_bank[t][:], ALU.add, ALU.mult)
 
         def hazard(t):
-            nc.scalar.activation(haz[t][:], ln_haz[t][:], ACT.Exp)
+            nc.scalar.activation(haz[t][:], ln_haz[t][:], ACT.Exp, bias=-math.log(2.0))
 
         def fetch_on_vector(t):
-            nc.gpsimd.tensor_scalar(haz[t][:], haz[t][:], half_unit[:, t : t + 1], 0.0, ALU.mult, ALU.add)
+            nc.gpsimd.tensor_scalar(haz[t][:], haz[t][:], unit_sb[:, t : t + 1], 0.0, ALU.mult, ALU.add)
             nc.vector.tensor_tensor(hv[:, t, :], volu[t][:].indirect(prv_sb[:]), haz[t][:], ALU.mult)
 
         vp = {t: sb.tile([P, S], F32, name="vp%d" % t) for t in (2, 3)}
@@ -242,7 +224,7 @@ def tile_picked_yacddu_haz_p_kernel(
             picks = prv_sb[:, h * (HALF // 16) : (h + 1) * (HALF // 16)]
             nc.scalar.activation(vp[t][:, cols], volu[t][:].indirect(picks), ACT.Copy)
             nc.vector.scalar_tensor_tensor(
-                hv[:, t, cols], vp[t][:, cols], half_unit[:, t : t + 1], haz[t][:, cols], ALU.mult, ALU.mult
+                hv[:, t, cols], vp[t][:, cols], unit_sb[:, t : t + 1], haz[t][:, cols], ALU.mult, ALU.mult
             )
 
         hid = [sb.tile([P, HALF * PACK], BF16, name="hid%d" % h, align_bytes=64) for h in range(2)]
@@ -257,7 +239,7 @@ def tile_picked_yacddu_haz_p_kernel(
             codes = sb.tile([P, HALF], U32, name="codes%d" % h, align_bytes=64)
             plane = sb.tile([P, HALF], U8, name="plane%d" % h, align_bytes=64)
             nc.vector.quantize_mx(codes[:].bitcast(FP8X4), plane[:], hid[h][:])
-            o_bank = bank(BLOCKS + h, "o_%d" % h)
+            o_bank = bank(h, "o_%d" % h)
             nc.tensor.matmul_mx(
                 o_bank[:, :HALF],
                 lhsT=w3w[:].bitcast(FP4X4),
@@ -271,9 +253,10 @@ def tile_picked_yacddu_haz_p_kernel(
             nc.scalar.copy(res[:], o_bank[:, :HALF])
             nc.sync.dma_start(out=out[:, h * HALF : (h + 1) * HALF], in_=res[:])
 
+        hazard(0)
         for t in (0, 1):
-            hazard(t)
             gate(t)
+        hazard(1)
         fetch_on_vector(0)
         for t in (2, 3):
             gate(t)

import math
from contextlib import ExitStack

import concourse.mybir as mybir
from concourse.masks import make_identity

F32 = mybir.dt.float32
BF16 = mybir.dt.bfloat16
I32 = mybir.dt.int32
U32 = mybir.dt.uint32
U16 = mybir.dt.uint16
U8 = mybir.dt.uint8
FP8X4 = mybir.dt.float8_e4m3fn_x4
FP4X4 = mybir.dt.float4_e2m1fn_x4
ACT = mybir.ActivationFunctionType
ALU = mybir.AluOpType

K, T, S, N, H = 1024, 1024, 512, 128, 512
P = 128
PACK = 4
PASSES = K // (P * PACK)
QUADS = 4
BLOCKS = S // P
HALF = S // 2
FLOPS = 2 * (2 * K * H * S) + 2 * H * N * S

KNEE = 30.0
PSI_SHIFT = 0.25


def tile_picked_yacddu_haz_p_kernel(
    tc, x_words, x_scales, w1_words, w1_scales, w2_words, w2_scales, eps, unit, w3_words, w3_scales, offs, prv, out
):
    nc = tc.nc
    with ExitStack() as ctx:
        lists = ctx.enter_context(tc.tile_pool(name="lists", bufs=1))
        sb = ctx.enter_context(tc.tile_pool(name="sb", bufs=1))
        psum = ctx.enter_context(tc.psum_pool(name="psum", bufs=1))

        def bank(b, name):
            return psum.tile([P, S], F32, name=name, tag="bank%d" % b)

        def load_scale_rows(queue, plane, scales):
            for q in range(QUADS):
                queue.dma_start(
                    out=plane[32 * q : 32 * q + 4].bitcast(I32),
                    in_=scales[:, 4 * q : 4 * q + 4, :].rearrange("o r c -> r o c").bitcast(I32),
                )

        offs_sb = lists.tile([P, S // 16], U16, name="offs_sb")
        prv_sb = lists.tile([P, S // 16], U16, name="prv_sb")
        xw = sb.tile([P, PASSES, T], U32, name="xw")
        xs = sb.tile([P, PASSES, T], U8, name="xs", tag="xs")
        ww = [sb.tile([P, PASSES, 2 * H], U8, name="ww%d" % i, align_bytes=64) for i in range(2)]
        ws = [sb.tile([P, PASSES, H], U8, name="ws%d" % i, align_bytes=64) for i in range(2)]
        w3w = sb.tile([P, 2 * N], U8, name="w3w", align_bytes=64)
        w3s = sb.tile([P, 1, N], U8, name="w3s", align_bytes=64)
        unit_sb = sb.tile([P, PACK], F32, name="unit_sb")
        eps_sb = sb.tile([P, PACK, S], F32, name="eps_sb")
        ident = sb.tile([P, P], F32, name="ident")

        nc.gpsimd.memset(xs[:].bitcast(I32), 0)
        for plane in (ws[0], ws[1], w3s):
            nc.vector.memset(plane[:].bitcast(I32), 0)

        def load_w_words(i, words):
            nc.sync.dma_start(out=ww[i][:].bitcast(I32), in_=words.rearrange("o p c -> p o c").bitcast(I32))

        nc.sync.dma_start(offs_sb[:], offs)
        nc.sync.dma_start(prv_sb[:], prv)
        nc.sync.dma_start(out=w3w[:].bitcast(I32), in_=w3_words[0].bitcast(I32))
        load_scale_rows(nc.sync, xs, x_scales)
        nc.sync.dma_start(out=xw[:].bitcast(I32), in_=x_words.rearrange("o p c r -> p o (c r)").bitcast(I32))
        load_w_words(0, w1_words)
        load_scale_rows(nc.sync, ws[0], w1_scales)
        load_w_words(1, w2_words)
        load_scale_rows(nc.sync, ws[1], w2_scales)
        nc.sync.dma_start(out=eps_sb[:], in_=eps.rearrange("(p t) j -> p t j", t=PACK))
        nc.sync.dma_start(out=unit_sb[:], in_=unit.rearrange("(p t) o -> p (t o)", t=PACK))
        load_scale_rows(nc.sync, w3s, w3_scales)
        make_identity(nc, ident[:])

        def dealt(ap):
            return ap.rearrange("p (m t) -> p t m", t=PACK)

        e1 = [sb.tile([P, PACK, P], F32, name="e1_%d" % b) for b in range(BLOCKS)]
        r1 = [sb.tile([P, PACK, P], F32, name="r1_%d" % b) for b in range(BLOCKS)]
        r2 = [sb.tile([P, PACK, P], F32, name="r2_%d" % b) for b in range(BLOCKS)]
        l2 = [sb.tile([P, PACK, P], F32, name="l2_%d" % b) for b in range(BLOCKS)]
        e2 = sb.tile([P, BLOCKS, PACK, P], F32, name="e2")

        gs = [sb.tile([P, S], U8, name="gs%d" % o, align_bytes=64) for o in range(PASSES)]
        gw = [
            [sb.tile([P, P], U32, name="gw%d_%d" % (b, o), tag="gw%d_%d" % (b, o), align_bytes=64) for o in range(PASSES)]
            for b in range(BLOCKS)
        ]

        def pick_words(b, o):
            nc.vector.tensor_copy(gw[b][o][:], xw[:, o, :].indirect(offs_sb[:, b * (P // 16) : (b + 1) * (P // 16)]))

        for o in range(PASSES):
            nc.vector.tensor_copy(gs[o][:], xs[:, o, :].indirect(offs_sb[:]))
        for b in range(BLOCKS):
            for o in range(PASSES):
                pick_words(b, o)

        def mx_pass(acc, i, b, o):
            nc.tensor.matmul_mx(
                acc[:],
                lhsT=gw[b][o][:].bitcast(FP8X4),
                lhsT_scale=gs[o][:, b * P : (b + 1) * P],
                rhs=ww[i][:, o, :].bitcast(FP4X4),
                rhs_scale=ws[i][:, o, :],
                start=(o == 0),
                stop=(o == PASSES - 1),
            )

        y_bank = [bank(b, "y_%d" % b) for b in range(BLOCKS)]
        v_bank = [bank(BLOCKS + b, "v_%d" % b) for b in range(BLOCKS)]
        for b in range(BLOCKS):
            for o in range(PASSES):
                mx_pass(y_bank[b], 0, b, o)
            nc.scalar.activation(e1[b][:], dealt(y_bank[b][:]), ACT.Exp)
            nc.gpsimd.tensor_scalar(e1[b][:], e1[b][:], math.exp(KNEE), 0.0, ALU.min, ALU.max)
        for b in range(BLOCKS):
            for o in range(PASSES):
                mx_pass(v_bank[b], 1, b, o)
            nc.scalar.activation(e2[:, b], dealt(v_bank[b][:]), ACT.Exp)
        nc.gpsimd.tensor_scalar(e2[:], e2[:], math.exp(KNEE), 0.0, ALU.min, ALU.max)
        for b in range(BLOCKS):
            nc.vector.tensor_scalar(r1[b][:], dealt(y_bank[b][:]), -KNEE, 0.0, ALU.add, ALU.max)
        for b in range(BLOCKS):
            nc.vector.tensor_scalar(r2[b][:], dealt(v_bank[b][:]), -KNEE, 0.0, ALU.add, ALU.max)

        nc.vector.tensor_scalar(eps_sb[:], eps_sb[:], 0.6, None, ALU.mult)

        def flip(dst, src, start, stop):
            for b in range(BLOCKS):
                cols = slice(b * P, (b + 1) * P)
                nc.tensor.matmul(
                    dst[:, cols],
                    lhsT=src[:, cols],
                    rhs=ident[:],
                    is_transpose=True,
                    start=(start and b == 0),
                    stop=(stop and b == BLOCKS - 1),
                )

        def turn(dst, t, *sources):
            for b in range(BLOCKS):
                for i, src in enumerate(sources):
                    nc.tensor.matmul(
                        dst[:, b * P : (b + 1) * P],
                        lhsT=src[b][:, t, :],
                        rhs=ident[:],
                        is_transpose=True,
                        start=(i == 0),
                        stop=(i == len(sources) - 1),
                    )

        shift = math.exp(PSI_SHIFT)
        e_bank = [bank(t, "e_%d" % t) for t in range(PACK)]
        r_bank = [bank(BLOCKS + t, "r_%d" % t) for t in range(PACK)]
        psi = [sb.tile([P, 2 * S], F32, name="psi%d" % t, tag="psi%d" % t) for t in range(PACK)]
        dur = [sb.tile([P, S], F32, name="dur%d" % t) for t in range(PACK)]
        mix = []
        for t in range(PACK):
            turn(e_bank[t], t, e1)
            turn(r_bank[t], t, r1)
            nc.scalar.activation(psi[t][:, S:], e_bank[t][:], ACT.Ln, bias=shift, scale=shift)
        for step in range(PACK + 1):
            if step < PACK:
                t = step
                nc.vector.tensor_tensor(psi[t][:, :S], r_bank[t][:], psi[t][:, S:], ALU.add)
                mix.append(bank(BLOCKS + t, "mix_%d" % t))
                flip(mix[t], psi[t], True, False)
            if step >= 1:
                t = step - 1
                nc.vector.tensor_tensor(dur[t][:], psi[t][:].indirect(prv_sb[:]), eps_sb[:, t, :], ALU.mult)
                flip(mix[t], dur[t], False, True)

        for b in range(BLOCKS):
            nc.scalar.activation(l2[b][:], e2[:, b], ACT.Ln, bias=1.0)

        ln_dur, ln_psin = [], []
        for t in range(PACK):
            ln_dur.append(sb.tile([P, S], F32, name="ln_dur%d" % t, tag="ln_dur%d" % t))
            flipped = sb.tile([P, S], F32, name="flipped%d" % t)
            nc.scalar.activation(ln_dur[t][:], dur[t][:], ACT.Ln, bias=2.0**-63, scale=0.8 / 0.6)
            nc.scalar.activation(flipped[:], mix[t][:], ACT.Ln, bias=0.1, scale=0.4)
            ln_psin.append(bank(BLOCKS + t, "ln_psin%d" % t))
            flip(ln_psin[t], flipped, True, True)

        ln_haz = []
        for t in range(PACK):
            tag = "psi%d" % (PACK - 1) if t == 0 else "ln_dur%d" % (t - 1)
            ln_haz.append(sb.tile([P, S], F32, name="ln_haz%d" % t, tag=tag))
            nc.vector.scalar_tensor_tensor(ln_haz[t][:], ln_dur[t][:], 0.5, ln_psin[t][:], ALU.mult, ALU.subtract)

        s_bank = []
        for t in range(PACK):
            s_bank.append(bank(BLOCKS + t, "s_%d" % t))
            turn(s_bank[t], t, r2, l2)

        hv = sb.tile([P, PACK, S], F32, name="hv")
        volu = [sb.tile([P, 2 * S], F32, name="volu%d" % t) for t in range(PACK)]
        haz = [sb.tile([P, S], F32, name="haz%d" % t) for t in range(PACK)]

        def gate(t):
            nc.scalar.activation(volu[t][:, S:], ln_haz[t][:], ACT.Tanh, bias=-0.5 * math.log(0.7), scale=0.5)
            nc.vector.scalar_tensor_tensor(volu[t][:, :S], volu[t][:, S:], 1.0, s_bank[t][:], ALU.add, ALU.mult)

        def hazard(t):
            nc.scalar.activation(haz[t][:], ln_haz[t][:], ACT.Exp, bias=-math.log(2.0))

        def fetch_on_vector(t):
            nc.gpsimd.tensor_scalar(haz[t][:], haz[t][:], unit_sb[:, t : t + 1], 0.0, ALU.mult, ALU.add)
            nc.vector.tensor_tensor(hv[:, t, :], volu[t][:].indirect(prv_sb[:]), haz[t][:], ALU.mult)

        vp = {t: sb.tile([P, S], F32, name="vp%d" % t) for t in (2, 3)}

        def fetch_on_scalar(t, h):
            cols = slice(h * HALF, (h + 1) * HALF)
            picks = prv_sb[:, h * (HALF // 16) : (h + 1) * (HALF // 16)]
            nc.scalar.activation(vp[t][:, cols], volu[t][:].indirect(picks), ACT.Copy)
            nc.vector.scalar_tensor_tensor(
                hv[:, t, cols], vp[t][:, cols], unit_sb[:, t : t + 1], haz[t][:, cols], ALU.mult, ALU.mult
            )

        hid = [sb.tile([P, HALF * PACK], BF16, name="hid%d" % h, align_bytes=64) for h in range(2)]

        def weave(copy, h, first, count):
            copy(
                hid[h][:, first * PACK : (first + count) * PACK].rearrange("p (c i t) -> p c t i", i=4, t=PACK),
                hv[:, :, h * HALF + first : h * HALF + first + count].rearrange("p t (c i) -> p c t i", i=4),
            )

        def finish(h):
            codes = sb.tile([P, HALF], U32, name="codes%d" % h, align_bytes=64)
            plane = sb.tile([P, HALF], U8, name="plane%d" % h, align_bytes=64)
            nc.vector.quantize_mx(codes[:].bitcast(FP8X4), plane[:], hid[h][:])
            o_bank = bank(h, "o_%d" % h)
            nc.tensor.matmul_mx(
                o_bank[:, :HALF],
                lhsT=w3w[:].bitcast(FP4X4),
                lhsT_scale=w3s[:, 0, :],
                rhs=codes[:].bitcast(FP8X4),
                rhs_scale=plane[:],
                start=True,
                stop=True,
            )
            res = sb.tile([P, HALF], F32, name="res%d" % h)
            nc.scalar.copy(res[:], o_bank[:, :HALF])
            nc.sync.dma_start(out=out[:, h * HALF : (h + 1) * HALF], in_=res[:])

        hazard(0)
        for t in (0, 1):
            gate(t)
        hazard(1)
        fetch_on_vector(0)
        for t in (2, 3):
            gate(t)
        fetch_on_vector(1)
        for t in (2, 3):
            hazard(t)
        for t in (2, 3):
            fetch_on_scalar(t, 0)
        fetch_on_scalar(2, 1)
        weave(nc.vector.tensor_copy, 0, 0, HALF)
        fetch_on_scalar(3, 1)
        finish(0)
        weave(nc.scalar.copy, 1, 0, HALF // 2)
        weave(nc.vector.tensor_copy, 1, HALF // 2, HALF // 2)
        finish(1)
